import numpy as np
import ml_dtypes


def mxq(x, axis, fmt="e4m3"):
    dtype, down = {"e4m3": (ml_dtypes.float8_e4m3fn, 7), "e5m2": (ml_dtypes.float8_e5m2, 14)}[fmt]
    v = np.moveaxis(np.asarray(x, np.float32).astype(ml_dtypes.bfloat16).astype(np.float64), axis, -1)
    blocks = v.reshape(v.shape[:-1] + (-1, 32))
    amax = np.abs(blocks).max(-1, keepdims=True)
    byte = np.maximum(np.where(amax > 0, np.frexp(amax)[1] - 1 + 127, 0) - down, 1)
    scale = np.exp2(byte - 127.0)
    codes = (blocks / scale).astype(np.float32).astype(dtype).astype(np.float64)
    return np.moveaxis((codes * scale).reshape(v.shape), -1, axis)


WIDE = False


def mx_kscale(k):
    if not WIDE:
        return np.ones(k)
    levels = np.array([10, -10, 5, -5, 0])
    if k % 512:
        return np.exp2(np.random.permutation(np.resize(levels, k // 32))).repeat(32)
    a = np.empty((k // 512, 16))
    for p in range(k // 512):
        a[p, :8] = np.random.permutation(np.resize(levels, 8))
        for g in range(8):
            far = levels[np.abs(levels - a[p, g]) >= 10]
            a[p, g + 8] = far[np.random.randint(len(far))]
    return np.exp2(a.ravel()).repeat(32)


def f64(x):
    return np.asarray(x).astype(np.float64)


E2M1 = np.array([0.0, 0.5, 1.0, 1.5, 2.0, 3.0, 4.0, 6.0, -0.0, -0.5, -1.0, -1.5, -2.0, -3.0, -4.0, -6.0])


def pack_weight(w, fmt):
    k, n = w.shape
    w = f64(np.asarray(w, np.float32).astype(ml_dtypes.bfloat16)).reshape(k // 32, 32, n)
    amax = np.abs(w).max(1)
    if fmt == "e4m3":
        byte = np.frexp(amax)[1] - 1 + 127 - 7
    else:
        mant, ex = np.frexp(amax / 6.0)
        byte = np.where(mant > 0.5, ex, ex - 1) + 127
    byte = np.clip(np.where(amax > 0, byte, 1), 1, 254)
    scaled = (w * np.exp2(127.0 - byte)[:, None, :]).reshape(k, n).astype(np.float32)
    by_word = np.ascontiguousarray(scaled.reshape(k // 512, 128, 4, n).transpose(0, 1, 3, 2))
    if fmt == "e4m3":
        words = by_word.astype(ml_dtypes.float8_e4m3fn).view(np.uint8)
    else:
        c = by_word.astype(ml_dtypes.float4_e2m1fn).view(np.uint8) & 0xF
        words = (c[..., 0::2] | (c[..., 1::2] << 4)).reshape(k // 512, 128, 2 * n)
    return np.ascontiguousarray(words), np.ascontiguousarray(byte.astype(np.uint8).reshape(k // 512, 16, n))


def unpack_weight(words, scales, fmt):
    g, _, n = scales.shape
    words = np.ascontiguousarray(words).reshape(g, 128, n, -1)
    if fmt == "e4m3":
        vals = words.view(ml_dtypes.float8_e4m3fn).astype(np.float64)
    else:
        nib = np.empty((g, 128, n, 4), np.uint8)
        nib[..., 0::2] = words & 0xF
        nib[..., 1::2] = words >> 4
        vals = E2M1[nib]
    vals = vals * np.repeat(np.exp2(scales.astype(np.float64) - 127.0), 8, axis=1)[..., None]
    return vals.transpose(0, 1, 3, 2).reshape(g * 512, n)


def bf(x):
    return np.asarray(x, np.float32).astype(ml_dtypes.bfloat16)


def planes(Y):
    r, m = Y.shape
    b = f64(bf(Y)).reshape(r // 32, 32, m)
    amax = np.abs(b).max(1)
    byte = np.clip(np.where(amax > 0, np.frexp(amax)[1] - 1 + 127 - 7, 1), 1, 254)
    codes = (b * np.exp2(127.0 - byte)[:, None, :]).reshape(r, m).astype(np.float32).astype(ml_dtypes.float8_e4m3fn).view(np.uint8)
    words = codes.reshape(r // 512, 128, 4, m).transpose(0, 1, 3, 2)
    return np.ascontiguousarray(words), np.ascontiguousarray(byte.astype(np.uint8).reshape(r // 512, 16, m))


K, T, R, N = 1024, 512, 512, 512


def setup_inputs():
    n = np.random.standard_normal
    fk = mx_kscale(K)
    fr = mx_kscale(R)
    xtp = pack_weight(n((K, T)) / fk[:, None], "e2m1")
    wap = pack_weight(n((K, R)) * 1 / np.sqrt(K) * fk[:, None] * fr, "e4m3")
    wbp = pack_weight(n((R, N)) * 1 / np.sqrt(R) / fr[:, None], "e2m1")
    wyp = pack_weight(n((K, N)) * 1 / np.sqrt(K) * fk[:, None], "e4m3")
    return {
        "xt_words": xtp[0],
        "xt_scales": xtp[1],
        "wa_words": wap[0],
        "wa_scales": wap[1],
        "dc": (np.random.uniform(0.3, 0.9, (R, 1))).astype(np.float32),
        "wb_words": wbp[0],
        "wb_scales": wbp[1],
        "wy_words": wyp[0],
        "wy_scales": wyp[1],
    }


def reference(xt_words, xt_scales, wa_words, wa_scales, dc, wb_words, wb_scales, wy_words, wy_scales):
    xtu = unpack_weight(xt_words, xt_scales, "e2m1")
    wau = unpack_weight(wa_words, wa_scales, "e4m3")
    wbu = unpack_weight(wb_words, wb_scales, "e2m1")
    wyu = unpack_weight(wy_words, wy_scales, "e4m3")
    a = wau.T @ xtu
    h1 = np.maximum(a, 0.0)
    hp = np.pad(h1, ((0, 0), (1, 0)))[:, :T]
    hid = h1 + f64(dc) * hp
    hidq = mxq(hid, 0, "e4m3")
    y = wbu.T @ hidq + wyu.T @ xtu
    words, scales = planes(y)
    return y, words, scales

@@ -1,0 +1,235 @@
+from contextlib import ExitStack
+
+import concourse.mybir as mybir
+
+K, T, R, N = 1024, 512, 512, 512
+FLOPS = 2 * T * (K * R + R * N + K * N)
+
+F32 = mybir.dt.float32
+BF16 = mybir.dt.bfloat16
+I32 = mybir.dt.int32
+U8 = mybir.dt.uint8
+FP8X4 = mybir.dt.float8_e4m3fn_x4
+FP4X4 = mybir.dt.float4_e2m1fn_x4
+ALU = mybir.AluOpType
+
+P = 128
+PACK = 4
+CH = 128
+NCH = T // CH
+KP = K // 512
+
+
+def tile_mix_hidden_with_before_and_skip_pl_kernel(
+    tc, xt_words, xt_scales, wa_words, wa_scales, dc, wb_words, wb_scales, wy_words, wy_scales, out_0, out_1, out_2
+):
+    nc = tc.nc
+    with ExitStack() as ctx:
+        sb = ctx.enter_context(tc.tile_pool(name="sb", bufs=1))
+        ps = ctx.enter_context(tc.psum_pool(name="ps", bufs=1))
+        ctx.enter_context(tc.manual_schedule())
+
+        def tile(name, width, dtype):
+            return sb.tile([P, width], dtype, name=name, align_bytes=64)
+
+        xt_w = [tile("xt_w%d" % z, 2 * T, U8) for z in range(KP)]
+        xt_s = tile("xt_s", KP * T, U8)
+        wa_raw = [tile("wa_raw%d" % z, R, I32) for z in range(KP)]
+        wa_sraw = tile("wa_sraw", KP * R, U8)
+        wy_raw = [tile("wy_raw%d" % z, N, I32) for z in range(KP)]
+        wy_sraw = tile("wy_sraw", KP * N, U8)
+        wb_raw = tile("wb_raw", 2 * N, U8)
+        wb_sraw = tile("wb_sraw", N, U8)
+        wa_w = [tile("wa_w%d" % z, R, I32) for z in range(KP)]
+        wa_s = tile("wa_s", KP * R, U8)
+        wy_w = [tile("wy_w%d" % z, N, I32) for z in range(KP)]
+        wy_s = tile("wy_s", KP * N, U8)
+        wb_w = tile("wb_w", 2 * N, U8)
+        wb_s = tile("wb_s", N, U8)
+        dc_sb = tile("dc_sb", PACK, F32)
+        prev = tile("prev", PACK * (T + 1), F32)
+        hid = [tile("hid%d" % c, PACK * CH, BF16) for c in range(NCH)]
+        hq_w = [tile("hq_w%d" % c, CH, I32) for c in range(NCH)]
+        hq_s = [tile("hq_s%d" % c, CH, U8) for c in range(NCH)]
+        y32 = [tile("y32_%d" % c, PACK * CH, F32) for c in range(NCH)]
+        y16 = [tile("y16_%d" % c, PACK * CH, BF16) for c in range(NCH)]
+        yq_w = tile("yq_w", T, I32)
+        yq_s = tile("yq_s", T, U8)
+        a_ps = [ps.tile([P, PACK * CH], F32, name="a_ps%d" % c) for c in range(NCH)]
+        y_ps = [ps.tile([P, PACK * CH], F32, name="y_ps%d" % c) for c in range(NCH)]
+
+        def load_scales(eng, plane, src, q):
+            passes = src.shape[0]
+            eng.dma_start(
+                out=plane[32 * q : 32 * q + 4, :].bitcast(I32).rearrange("r (z n) -> r z n", z=passes),
+                in_=src[:, 4 * q : 4 * q + 4, :].bitcast(I32).rearrange("z r n -> r z n"),
+            )
+
+        def load_fp8(eng, dst, src, z):
+            eng.dma_start(out=dst[:], in_=src[z].rearrange("p n t -> p (n t)").bitcast(I32))
+
+        def load_fp4(eng, dst, src, z):
+            eng.dma_start(out=dst[:].bitcast(I32), in_=src[z].bitcast(I32))
+
+        nc.gpsimd.memset(wa_sraw[:].bitcast(I32), 0)
+        for plane in (xt_s, wb_sraw, wy_sraw):
+            nc.vector.memset(plane[:].bitcast(I32), 0)
+        nc.vector.memset(prev[:, 0:PACK], 0.0)
+
+        nc.gpsimd.dma_start(out=dc_sb[:], in_=dc.rearrange("(p j) o -> p (j o)", j=PACK))
+        for q in range(4):
+            load_scales(nc.gpsimd, wb_sraw, wb_scales, q)
+
+        load_scales(nc.sync, wa_sraw, wa_scales, 0)
+        load_scales(nc.scalar, wa_sraw, wa_scales, 1)
+        load_scales(nc.sync, wa_sraw, wa_scales, 2)
+        load_scales(nc.scalar, wa_sraw, wa_scales, 3)
+        load_scales(nc.sync, xt_s, xt_scales, 0)
+        load_scales(nc.scalar, xt_s, xt_scales, 1)
+        load_fp8(nc.sync, wa_raw[0], wa_words, 0)
+        load_fp4(nc.scalar, xt_w[0], xt_words, 0)
+        load_scales(nc.sync, xt_s, xt_scales, 2)
+        load_scales(nc.scalar, xt_s, xt_scales, 3)
+        load_fp8(nc.sync, wa_raw[1], wa_words, 1)
+        load_fp4(nc.scalar, xt_w[1], xt_words, 1)
+        load_fp8(nc.sync, wy_raw[0], wy_words, 0)
+        load_fp8(nc.sync, wy_raw[1], wy_words, 1)
+        load_fp4(nc.sync, wb_raw, wb_words, 0)
+        for q in range(4):
+            load_scales(nc.sync, wy_sraw, wy_scales, q)
+
+        def deal(dst, src, passes):
+            nc.vector.tensor_copy(
+                out=dst[:].rearrange("p (z j m) -> p z j m", z=passes, j=PACK),
+                in_=src[:].rearrange("p (z m j) -> p z j m", z=passes, j=PACK),
+            )
+
+        def deal_fp4(dst, src):
+            nc.vector.tensor_copy(
+                out=dst[:].rearrange("p (j m b) -> p j m b", j=PACK, b=2),
+                in_=src[:].rearrange("p (m j b) -> p j m b", j=PACK, b=2),
+            )
+
+        def x_pass(bank, w, s, z, j, c, start, stop):
+            nc.tensor.matmul_mx(
+                out=bank[:, j * CH : (j + 1) * CH],
+                lhsT=w[z][:, j * P : (j + 1) * P].bitcast(FP8X4),
+                lhsT_scale=s[:, z * 512 + j * P : z * 512 + (j + 1) * P],
+                rhs=xt_w[z][:, 2 * c * CH : 2 * (c + 1) * CH].bitcast(FP4X4),
+                rhs_scale=xt_s[:, z * T + c * CH : z * T + (c + 1) * CH],
+                start=start,
+                stop=stop,
+            )
+
+        def layer1(c):
+            for z in range(KP):
+                for j in range(PACK):
+                    x_pass(a_ps[c], wa_w, wa_s, z, j, c, z == 0 and j == 0, z == KP - 1 and j == PACK - 1)
+
+        def skip(c):
+            for z in range(KP):
+                for j in range(PACK):
+                    x_pass(y_ps[c], wy_w, wy_s, z, j, c, z == 0 and j == 0, False)
+
+        def layer2(c):
+            for j in range(PACK):
+                nc.tensor.matmul_mx(
+                    out=y_ps[c][:, j * CH : (j + 1) * CH],
+                    lhsT=wb_w[:, 2 * j * P : 2 * (j + 1) * P].bitcast(FP4X4),
+                    lhsT_scale=wb_s[:, j * P : (j + 1) * P],
+                    rhs=hq_w[c][:].bitcast(FP8X4),
+                    rhs_scale=hq_s[c][:],
+                    start=False,
+                    stop=(j == PACK - 1),
+                )
+
+        def by_token(bank):
+            return bank[:].rearrange("p (j t) -> p t j", j=PACK)
+
+        def words(ap):
+            return ap.rearrange("p (t j) -> p t j", j=PACK)
+
+        def scale_prev(c):
+            nc.vector.scalar_tensor_tensor(
+                out=words(prev[:, PACK * (c * CH + 1) : PACK * ((c + 1) * CH + 1)]),
+                in0=by_token(a_ps[c]),
+                scalar=0.0,
+                in1=dc_sb[:].unsqueeze(1).to_broadcast([P, CH, PACK]),
+                op0=ALU.max,
+                op1=ALU.mult,
+            )
+
+        def add_prev(c):
+            nc.vector.scalar_tensor_tensor(
+                out=words(hid[c][:]),
+                in0=by_token(a_ps[c]),
+                scalar=0.0,
+                in1=words(prev[:, PACK * c * CH : PACK * (c + 1) * CH]),
+                op0=ALU.max,
+                op1=ALU.add,
+            )
+
+        def quant_hid(c):
+            nc.vector.quantize_mx(out=hq_w[c][:].bitcast(FP8X4), scales=hq_s[c][:], in_=hid[c][:])
+
+        out_rows = out_0.rearrange("(p j) t -> p j t", j=PACK)
+        out_words = out_1[0].rearrange("p n t -> p (n t)").bitcast(I32)
+
+        def drain(c):
+            nc.scalar.copy(out=words(y16[c][:]), in_=by_token(y_ps[c]))
+            nc.scalar.copy(out=y32[c][:], in_=y_ps[c][:])
+            eng = nc.scalar if c == NCH - 1 else nc.sync
+            eng.dma_start(
+                out=out_rows[:, :, c * CH : (c + 1) * CH], in_=y32[c][:].rearrange("p (j t) -> p j t", j=PACK)
+            )
+
+        def quant_out(c):
+            cols = slice(c * CH, (c + 1) * CH)
+            nc.vector.quantize_mx(out=yq_w[:, cols].bitcast(FP8X4), scales=yq_s[:, cols], in_=y16[c][:])
+            nc.sync.dma_start(out=out_words[:, cols], in_=yq_w[:, cols])
+
+        deal(wa_s, wa_sraw, KP)
+        deal(wa_w[0], wa_raw[0], 1)
+        deal(wa_w[1], wa_raw[1], 1)
+        layer1(0)
+        layer1(1)
+        layer1(2)
+        deal(wy_w[0], wy_raw[0], 1)
+        deal(wy_w[1], wy_raw[1], 1)
+        scale_prev(0)
+        deal(wy_s, wy_sraw, KP)
+        skip(0)
+        add_prev(0)
+        deal_fp4(wb_w, wb_raw)
+        quant_hid(0)
+        scale_prev(1)
+        deal(wb_s, wb_sraw, 1)
+        layer1(3)
+        layer2(0)
+        drain(0)
+        skip(1)
+        add_prev(1)
+        scale_prev(2)
+        quant_hid(1)
+        layer2(1)
+        drain(1)
+        skip(2)
+        skip(3)
+        add_prev(2)
+        quant_out(0)
+        scale_prev(3)
+        quant_hid(2)
+        layer2(2)
+        drain(2)
+        add_prev(3)
+        quant_out(1)
+        quant_hid(3)
+        layer2(3)
+        quant_out(2)
+        drain(3)
+        quant_out(3)
+        for q in range(4):
+            eng = nc.sync if q < 2 else nc.scalar
+            eng.dma_start(
+                out=out_2[0, 4 * q : 4 * q + 4, :].bitcast(I32), in_=yq_s[32 * q : 32 * q + 4, :].bitcast(I32)
+            )

@@ -12,12 +12,15 @@ U8 = mybir.dt.uint8
 FP8X4 = mybir.dt.float8_e4m3fn_x4
 FP4X4 = mybir.dt.float4_e2m1fn_x4
 ALU = mybir.AluOpType
+ACT = mybir.ActivationFunctionType
 
 P = 128
 PACK = 4
 CH = 128
 NCH = T // CH
 KP = K // 512
+EARLY = 2
+HW = PACK + EARLY * CH
 
 
 def tile_mix_hidden_with_before_and_skip_pl_kernel(
@@ -47,7 +50,10 @@ def tile_mix_hidden_with_before_and_skip_pl_kernel(
         wb_w = tile("wb_w", 2 * N, U8)
         wb_s = tile("wb_s", N, U8)
         dc_sb = tile("dc_sb", PACK, F32)
-        prev = tile("prev", PACK * (T + 1), F32)
+        prev = tile("prev", PACK * ((NCH - EARLY) * CH + 1), F32)
+        h1 = tile("h1", PACK * HW, F32)
+        hb = [tile("hb%d" % c, PACK * CH, BF16) for c in range(EARLY)]
+        h1v = h1[:].rearrange("p (j t) -> p j t", j=PACK)
         hid = [tile("hid%d" % c, PACK * CH, BF16) for c in range(NCH)]
         hq_w = [tile("hq_w%d" % c, CH, I32) for c in range(NCH)]
         hq_s = [tile("hq_s%d" % c, CH, U8) for c in range(NCH)]
@@ -74,16 +80,14 @@ def tile_mix_hidden_with_before_and_skip_pl_kernel(
         nc.gpsimd.memset(wa_sraw[:].bitcast(I32), 0)
         for plane in (xt_s, wb_sraw, wy_sraw):
             nc.vector.memset(plane[:].bitcast(I32), 0)
-        nc.vector.memset(prev[:, 0:PACK], 0.0)
+        nc.vector.memset(h1v[:, :, PACK - 1 : PACK], 0.0)
 
         nc.gpsimd.dma_start(out=dc_sb[:], in_=dc.rearrange("(p j) o -> p (j o)", j=PACK))
         for q in range(4):
             load_scales(nc.gpsimd, wb_sraw, wb_scales, q)
 
-        load_scales(nc.sync, wa_sraw, wa_scales, 0)
-        load_scales(nc.scalar, wa_sraw, wa_scales, 1)
-        load_scales(nc.sync, wa_sraw, wa_scales, 2)
-        load_scales(nc.scalar, wa_sraw, wa_scales, 3)
+        for q in range(4):
+            load_scales(nc.sync if q % 2 == 0 else nc.scalar, wa_sraw, wa_scales, q)
         load_scales(nc.sync, xt_s, xt_scales, 0)
         load_scales(nc.scalar, xt_s, xt_scales, 1)
         load_fp8(nc.sync, wa_raw[0], wa_words, 0)
@@ -92,11 +96,17 @@ def tile_mix_hidden_with_before_and_skip_pl_kernel(
         load_scales(nc.scalar, xt_s, xt_scales, 3)
         load_fp8(nc.sync, wa_raw[1], wa_words, 1)
         load_fp4(nc.scalar, xt_w[1], xt_words, 1)
+        load_fp4(nc.sync, wb_raw, wb_words, 0)
         load_fp8(nc.sync, wy_raw[0], wy_words, 0)
         load_fp8(nc.sync, wy_raw[1], wy_words, 1)
-        load_fp4(nc.sync, wb_raw, wb_words, 0)
         for q in range(4):
             load_scales(nc.sync, wy_sraw, wy_scales, q)
+
+        def deal_words(dst, src):
+            nc.vector.tensor_copy(
+                out=dst[:].rearrange("p (j g m) -> p g j m", j=PACK, m=PACK),
+                in_=src[:].rearrange("p (g m j) -> p g j m", j=PACK, m=PACK),
+            )
 
         def deal(dst, src, passes):
             nc.vector.tensor_copy(
@@ -151,7 +161,7 @@ def tile_mix_hidden_with_before_and_skip_pl_kernel(
 
         def scale_prev(c):
             nc.vector.scalar_tensor_tensor(
-                out=words(prev[:, PACK * (c * CH + 1) : PACK * ((c + 1) * CH + 1)]),
+                out=words(prev[:, PACK * ((c - EARLY) * CH + 1) : PACK * ((c - EARLY + 1) * CH + 1)]),
                 in0=by_token(a_ps[c]),
                 scalar=0.0,
                 in1=dc_sb[:].unsqueeze(1).to_broadcast([P, CH, PACK]),
@@ -164,9 +174,39 @@ def tile_mix_hidden_with_before_and_skip_pl_kernel(
                 out=words(hid[c][:]),
                 in0=by_token(a_ps[c]),
                 scalar=0.0,
-                in1=words(prev[:, PACK * c * CH : PACK * (c + 1) * CH]),
+                in1=words(prev[:, PACK * (c - EARLY) * CH : PACK * (c - EARLY + 1) * CH]),
                 op0=ALU.max,
                 op1=ALU.add,
+            )
+
+        def relu(c):
+            nc.scalar.activation(
+                out=h1v[:, :, PACK + c * CH : PACK + (c + 1) * CH],
+                in_=a_ps[c][:].rearrange("p (j t) -> p j t", j=PACK),
+                func=ACT.Relu,
+            )
+
+        def blend(c):
+            for j in range(PACK):
+                t0 = j * HW + PACK + c * CH
+                nc.vector.scalar_tensor_tensor(
+                    out=hb[c][:, j * CH : (j + 1) * CH],
+                    in0=h1[:, t0 - 1 : t0 - 1 + CH],
+                    scalar=dc_sb[:, j : j + 1],
+                    in1=h1[:, t0 : t0 + CH],
+                    op0=ALU.mult,
+                    op1=ALU.add,
+                )
+
+        def carry():
+            nc.vector.tensor_tensor(
+                out=prev[:, 0:PACK], in0=h1[:, HW - 1 : PACK * HW : HW], in1=dc_sb[:], op=ALU.mult
+            )
+
+        def interleave(copy, dst, src):
+            copy(
+                out=dst[:].rearrange("p (g m j) -> p g j m", j=PACK, m=PACK),
+                in_=src[:].rearrange("p (j g m) -> p g j m", j=PACK, m=PACK),
             )
 
         def quant_hid(c):
@@ -175,8 +215,10 @@ def tile_mix_hidden_with_before_and_skip_pl_kernel(
         out_rows = out_0.rearrange("(p j) t -> p j t", j=PACK)
         out_words = out_1[0].rearrange("p n t -> p (n t)").bitcast(I32)
 
-        def drain(c):
+        def round_out(c):
             nc.scalar.copy(out=words(y16[c][:]), in_=by_token(y_ps[c]))
+
+        def drain(c):
             nc.scalar.copy(out=y32[c][:], in_=y_ps[c][:])
             eng = nc.scalar if c == NCH - 1 else nc.sync
             eng.dma_start(
@@ -186,48 +228,60 @@ def tile_mix_hidden_with_before_and_skip_pl_kernel(
         def quant_out(c):
             cols = slice(c * CH, (c + 1) * CH)
             nc.vector.quantize_mx(out=yq_w[:, cols].bitcast(FP8X4), scales=yq_s[:, cols], in_=y16[c][:])
+
+        def store_words(cols):
             nc.sync.dma_start(out=out_words[:, cols], in_=yq_w[:, cols])
 
         deal(wa_s, wa_sraw, KP)
-        deal(wa_w[0], wa_raw[0], 1)
-        deal(wa_w[1], wa_raw[1], 1)
+        deal_words(wa_w[0], wa_raw[0])
+        deal_words(wa_w[1], wa_raw[1])
+        deal_fp4(wb_w, wb_raw)
         layer1(0)
+        relu(0)
         layer1(1)
+        relu(1)
         layer1(2)
-        deal(wy_w[0], wy_raw[0], 1)
-        deal(wy_w[1], wy_raw[1], 1)
-        scale_prev(0)
+        layer1(3)
+        deal_words(wy_w[0], wy_raw[0])
+        deal_words(wy_w[1], wy_raw[1])
+        blend(0)
+        interleave(nc.scalar.copy, hid[0], hb[0])
         deal(wy_s, wy_sraw, KP)
         skip(0)
-        add_prev(0)
-        deal_fp4(wb_w, wb_raw)
+        blend(1)
+        interleave(nc.scalar.copy, hid[1], hb[1])
         quant_hid(0)
-        scale_prev(1)
         deal(wb_s, wb_sraw, 1)
-        layer1(3)
         layer2(0)
+        round_out(0)
         drain(0)
         skip(1)
-        add_prev(1)
+        carry()
         scale_prev(2)
         quant_hid(1)
         layer2(1)
         drain(1)
+        round_out(1)
         skip(2)
-        skip(3)
         add_prev(2)
-        quant_out(0)
         scale_prev(3)
         quant_hid(2)
         layer2(2)
         drain(2)
+        skip(3)
         add_prev(3)
-        quant_out(1)
+        quant_out(0)
+        store_words(slice(0, CH))
         quant_hid(3)
         layer2(3)
+        interleave(nc.vector.tensor_copy, y16[2], y32[2])
+        quant_out(1)
+        round_out(3)
         quant_out(2)
+        store_words(slice(CH, 3 * CH))
         drain(3)
         quant_out(3)
+        store_words(slice(3 * CH, T))
         for q in range(4):
             eng = nc.sync if q < 2 else nc.scalar
             eng.dma_start(

from contextlib import ExitStack

import concourse.mybir as mybir

K, T, R, N = 1024, 512, 512, 512
FLOPS = 2 * T * (K * R + R * N + K * N)

F32 = mybir.dt.float32
BF16 = mybir.dt.bfloat16
I32 = mybir.dt.int32
U8 = mybir.dt.uint8
FP8X4 = mybir.dt.float8_e4m3fn_x4
FP4X4 = mybir.dt.float4_e2m1fn_x4
ALU = mybir.AluOpType
ACT = mybir.ActivationFunctionType

P = 128
PACK = 4
CH = 128
NCH = T // CH
KP = K // 512
EARLY = 2
HW = PACK + EARLY * CH


def tile_mix_hidden_with_before_and_skip_pl_kernel(
    tc, xt_words, xt_scales, wa_words, wa_scales, dc, wb_words, wb_scales, wy_words, wy_scales, out_0, out_1, out_2
):
    nc = tc.nc
    with ExitStack() as ctx:
        sb = ctx.enter_context(tc.tile_pool(name="sb", bufs=1))
        ps = ctx.enter_context(tc.psum_pool(name="ps", bufs=1))
        ctx.enter_context(tc.manual_schedule())

        def tile(name, width, dtype):
            return sb.tile([P, width], dtype, name=name, align_bytes=64)

        xt_w = [tile("xt_w%d" % z, 2 * T, U8) for z in range(KP)]
        xt_s = tile("xt_s", KP * T, U8)
        wa_raw = [tile("wa_raw%d" % z, R, I32) for z in range(KP)]
        wa_sraw = tile("wa_sraw", KP * R, U8)
        wy_raw = [tile("wy_raw%d" % z, N, I32) for z in range(KP)]
        wy_sraw = tile("wy_sraw", KP * N, U8)
        wb_raw = tile("wb_raw", 2 * N, U8)
        wb_sraw = tile("wb_sraw", N, U8)
        wa_w = [tile("wa_w%d" % z, R, I32) for z in range(KP)]
        wa_s = tile("wa_s", KP * R, U8)
        wy_w = [tile("wy_w%d" % z, N, I32) for z in range(KP)]
        wy_s = tile("wy_s", KP * N, U8)
        wb_w = tile("wb_w", 2 * N, U8)
        wb_s = tile("wb_s", N, U8)
        dc_sb = tile("dc_sb", PACK, F32)
        prev = tile("prev", PACK * ((NCH - EARLY) * CH + 1), F32)
        h1 = tile("h1", PACK * HW, F32)
        hb = [tile("hb%d" % c, PACK * CH, BF16) for c in range(EARLY)]
        h1v = h1[:].rearrange("p (j t) -> p j t", j=PACK)
        hid = [tile("hid%d" % c, PACK * CH, BF16) for c in range(NCH)]
        hq_w = [tile("hq_w%d" % c, CH, I32) for c in range(NCH)]
        hq_s = [tile("hq_s%d" % c, CH, U8) for c in range(NCH)]
        y32 = [tile("y32_%d" % c, PACK * CH, F32) for c in range(NCH)]
        y16 = [tile("y16_%d" % c, PACK * CH, BF16) for c in range(NCH)]
        yq_w = tile("yq_w", T, I32)
        yq_s = tile("yq_s", T, U8)
        a_ps = [ps.tile([P, PACK * CH], F32, name="a_ps%d" % c) for c in range(NCH)]
        y_ps = [ps.tile([P, PACK * CH], F32, name="y_ps%d" % c) for c in range(NCH)]

        def load_scales(eng, plane, src, q):
            passes = src.shape[0]
            eng.dma_start(
                out=plane[32 * q : 32 * q + 4, :].bitcast(I32).rearrange("r (z n) -> r z n", z=passes),
                in_=src[:, 4 * q : 4 * q + 4, :].bitcast(I32).rearrange("z r n -> r z n"),
            )

        def load_fp8(eng, dst, src, z):
            eng.dma_start(out=dst[:], in_=src[z].rearrange("p n t -> p (n t)").bitcast(I32))

        def load_fp4(eng, dst, src, z):
            eng.dma_start(out=dst[:].bitcast(I32), in_=src[z].bitcast(I32))

        nc.gpsimd.memset(wa_sraw[:].bitcast(I32), 0)
        for plane in (xt_s, wb_sraw, wy_sraw):
            nc.vector.memset(plane[:].bitcast(I32), 0)
        nc.vector.memset(h1v[:, :, PACK - 1 : PACK], 0.0)

        nc.gpsimd.dma_start(out=dc_sb[:], in_=dc.rearrange("(p j) o -> p (j o)", j=PACK))
        for q in range(4):
            load_scales(nc.gpsimd, wb_sraw, wb_scales, q)

        for q in range(4):
            load_scales(nc.sync if q % 2 == 0 else nc.scalar, wa_sraw, wa_scales, q)
        load_scales(nc.sync, xt_s, xt_scales, 0)
        load_scales(nc.scalar, xt_s, xt_scales, 1)
        load_fp8(nc.sync, wa_raw[0], wa_words, 0)
        load_fp4(nc.scalar, xt_w[0], xt_words, 0)
        load_scales(nc.sync, xt_s, xt_scales, 2)
        load_scales(nc.scalar, xt_s, xt_scales, 3)
        load_fp8(nc.sync, wa_raw[1], wa_words, 1)
        load_fp4(nc.scalar, xt_w[1], xt_words, 1)
        load_fp4(nc.sync, wb_raw, wb_words, 0)
        load_fp8(nc.sync, wy_raw[0], wy_words, 0)
        load_fp8(nc.sync, wy_raw[1], wy_words, 1)
        for q in range(4):
            load_scales(nc.sync, wy_sraw, wy_scales, q)

        def deal_words(dst, src):
            nc.vector.tensor_copy(
                out=dst[:].rearrange("p (j g m) -> p g j m", j=PACK, m=PACK),
                in_=src[:].rearrange("p (g m j) -> p g j m", j=PACK, m=PACK),
            )

        def deal(dst, src, passes):
            nc.vector.tensor_copy(
                out=dst[:].rearrange("p (z j m) -> p z j m", z=passes, j=PACK),
                in_=src[:].rearrange("p (z m j) -> p z j m", z=passes, j=PACK),
            )

        def deal_fp4(dst, src):
            nc.vector.tensor_copy(
                out=dst[:].rearrange("p (j m b) -> p j m b", j=PACK, b=2),
                in_=src[:].rearrange("p (m j b) -> p j m b", j=PACK, b=2),
            )

        def x_pass(bank, w, s, z, j, c, start, stop):
            nc.tensor.matmul_mx(
                out=bank[:, j * CH : (j + 1) * CH],
                lhsT=w[z][:, j * P : (j + 1) * P].bitcast(FP8X4),
                lhsT_scale=s[:, z * 512 + j * P : z * 512 + (j + 1) * P],
                rhs=xt_w[z][:, 2 * c * CH : 2 * (c + 1) * CH].bitcast(FP4X4),
                rhs_scale=xt_s[:, z * T + c * CH : z * T + (c + 1) * CH],
                start=start,
                stop=stop,
            )

        def layer1(c):
            for z in range(KP):
                for j in range(PACK):
                    x_pass(a_ps[c], wa_w, wa_s, z, j, c, z == 0 and j == 0, z == KP - 1 and j == PACK - 1)

        def skip(c):
            for z in range(KP):
                for j in range(PACK):
                    x_pass(y_ps[c], wy_w, wy_s, z, j, c, z == 0 and j == 0, False)

        def layer2(c):
            for j in range(PACK):
                nc.tensor.matmul_mx(
                    out=y_ps[c][:, j * CH : (j + 1) * CH],
                    lhsT=wb_w[:, 2 * j * P : 2 * (j + 1) * P].bitcast(FP4X4),
                    lhsT_scale=wb_s[:, j * P : (j + 1) * P],
                    rhs=hq_w[c][:].bitcast(FP8X4),
                    rhs_scale=hq_s[c][:],
                    start=False,
                    stop=(j == PACK - 1),
                )

        def by_token(bank):
            return bank[:].rearrange("p (j t) -> p t j", j=PACK)

        def words(ap):
            return ap.rearrange("p (t j) -> p t j", j=PACK)

        def scale_prev(c):
            nc.vector.scalar_tensor_tensor(
                out=words(prev[:, PACK * ((c - EARLY) * CH + 1) : PACK * ((c - EARLY + 1) * CH + 1)]),
                in0=by_token(a_ps[c]),
                scalar=0.0,
                in1=dc_sb[:].unsqueeze(1).to_broadcast([P, CH, PACK]),
                op0=ALU.max,
                op1=ALU.mult,
            )

        def add_prev(c):
            nc.vector.scalar_tensor_tensor(
                out=words(hid[c][:]),
                in0=by_token(a_ps[c]),
                scalar=0.0,
                in1=words(prev[:, PACK * (c - EARLY) * CH : PACK * (c - EARLY + 1) * CH]),
                op0=ALU.max,
                op1=ALU.add,
            )

        def relu(c):
            nc.scalar.activation(
                out=h1v[:, :, PACK + c * CH : PACK + (c + 1) * CH],
                in_=a_ps[c][:].rearrange("p (j t) -> p j t", j=PACK),
                func=ACT.Relu,
            )

        def blend(c):
            for j in range(PACK):
                t0 = j * HW + PACK + c * CH
                nc.vector.scalar_tensor_tensor(
                    out=hb[c][:, j * CH : (j + 1) * CH],
                    in0=h1[:, t0 - 1 : t0 - 1 + CH],
                    scalar=dc_sb[:, j : j + 1],
                    in1=h1[:, t0 : t0 + CH],
                    op0=ALU.mult,
                    op1=ALU.add,
                )

        def carry():
            nc.vector.tensor_tensor(
                out=prev[:, 0:PACK], in0=h1[:, HW - 1 : PACK * HW : HW], in1=dc_sb[:], op=ALU.mult
            )

        def interleave(copy, dst, src):
            copy(
                out=dst[:].rearrange("p (g m j) -> p g j m", j=PACK, m=PACK),
                in_=src[:].rearrange("p (j g m) -> p g j m", j=PACK, m=PACK),
            )

        def quant_hid(c):
            nc.vector.quantize_mx(out=hq_w[c][:].bitcast(FP8X4), scales=hq_s[c][:], in_=hid[c][:])

        out_rows = out_0.rearrange("(p j) t -> p j t", j=PACK)
        out_words = out_1[0].rearrange("p n t -> p (n t)").bitcast(I32)

        def round_out(c):
            nc.scalar.copy(out=words(y16[c][:]), in_=by_token(y_ps[c]))

        def drain(c):
            nc.scalar.copy(out=y32[c][:], in_=y_ps[c][:])
            eng = nc.scalar if c == NCH - 1 else nc.sync
            eng.dma_start(
                out=out_rows[:, :, c * CH : (c + 1) * CH], in_=y32[c][:].rearrange("p (j t) -> p j t", j=PACK)
            )

        def quant_out(c):
            cols = slice(c * CH, (c + 1) * CH)
            nc.vector.quantize_mx(out=yq_w[:, cols].bitcast(FP8X4), scales=yq_s[:, cols], in_=y16[c][:])

        def store_words(cols):
            nc.sync.dma_start(out=out_words[:, cols], in_=yq_w[:, cols])

        deal(wa_s, wa_sraw, KP)
        deal_words(wa_w[0], wa_raw[0])
        deal_words(wa_w[1], wa_raw[1])
        deal_fp4(wb_w, wb_raw)
        layer1(0)
        relu(0)
        layer1(1)
        relu(1)
        layer1(2)
        layer1(3)
        deal_words(wy_w[0], wy_raw[0])
        deal_words(wy_w[1], wy_raw[1])
        blend(0)
        interleave(nc.scalar.copy, hid[0], hb[0])
        deal(wy_s, wy_sraw, KP)
        skip(0)
        blend(1)
        interleave(nc.scalar.copy, hid[1], hb[1])
        quant_hid(0)
        deal(wb_s, wb_sraw, 1)
        layer2(0)
        round_out(0)
        drain(0)
        skip(1)
        carry()
        scale_prev(2)
        quant_hid(1)
        layer2(1)
        drain(1)
        round_out(1)
        skip(2)
        add_prev(2)
        scale_prev(3)
        quant_hid(2)
        layer2(2)
        drain(2)
        skip(3)
        add_prev(3)
        quant_out(0)
        store_words(slice(0, CH))
        quant_hid(3)
        layer2(3)
        interleave(nc.vector.tensor_copy, y16[2], y32[2])
        quant_out(1)
        round_out(3)
        quant_out(2)
        store_words(slice(CH, 3 * CH))
        drain(3)
        quant_out(3)
        store_words(slice(3 * CH, T))
        for q in range(4):
            eng = nc.sync if q < 2 else nc.scalar
            eng.dma_start(
                out=out_2[0, 4 * q : 4 * q + 4, :].bitcast(I32), in_=yq_s[32 * q : 32 * q + 4, :].bitcast(I32)
            )
